import numpy as np
import ml_dtypes


def mxq(x, axis, fmt="e4m3"):
    dtype, down = {"e4m3": (ml_dtypes.float8_e4m3fn, 7), "e5m2": (ml_dtypes.float8_e5m2, 14)}[fmt]
    v = np.moveaxis(np.asarray(x, np.float32).astype(ml_dtypes.bfloat16).astype(np.float64), axis, -1)
    blocks = v.reshape(v.shape[:-1] + (-1, 32))
    amax = np.abs(blocks).max(-1, keepdims=True)
    byte = np.maximum(np.where(amax > 0, np.frexp(amax)[1] - 1 + 127, 0) - down, 1)
    scale = np.exp2(byte - 127.0)
    codes = (blocks / scale).astype(np.float32).astype(dtype).astype(np.float64)
    return np.moveaxis((codes * scale).reshape(v.shape), -1, axis)


WIDE = False


def mx_kscale(k):
    if not WIDE:
        return np.ones(k)
    levels = np.array([10, -10, 5, -5, 0])
    if k % 512:
        return np.exp2(np.random.permutation(np.resize(levels, k // 32))).repeat(32)
    a = np.empty((k // 512, 16))
    for p in range(k // 512):
        a[p, :8] = np.random.permutation(np.resize(levels, 8))
        for g in range(8):
            far = levels[np.abs(levels - a[p, g]) >= 10]
            a[p, g + 8] = far[np.random.randint(len(far))]
    return np.exp2(a.ravel()).repeat(32)


def f64(x):
    return np.asarray(x).astype(np.float64)


def striped8(idx):
    return np.concatenate([x.reshape(-1, 16).T for x in idx]).astype(np.uint16)


def runs(offs, k):
    lists = np.stack([offs[16 * r : 16 * r + 16].T.reshape(-1) for r in range(8)]).astype(np.int64)
    return lists[np.arange(k) % 512 // 64]


def pack_weight(w):
    k, n = w.shape
    w = f64(np.asarray(w, np.float32).astype(ml_dtypes.bfloat16)).reshape(k // 32, 32, n)
    amax = np.abs(w).max(1)
    byte = np.clip(np.where(amax > 0, np.frexp(amax)[1] - 1 + 127 - 7, 1), 1, 254)
    scaled = (w * np.exp2(127.0 - byte)[:, None, :]).reshape(k, n).astype(np.float32)
    words = np.ascontiguousarray(scaled.reshape(k // 512, 128, 4, n).transpose(0, 1, 3, 2)).astype(ml_dtypes.float8_e4m3fn).view(np.uint8)
    return words, np.ascontiguousarray(byte.astype(np.uint8).reshape(k // 512, 16, n))


def unpack_weight(words, scales):
    g, p, n, _ = words.shape
    vals = np.ascontiguousarray(words).view(ml_dtypes.float8_e4m3fn).astype(np.float64) * np.repeat(np.exp2(scales.astype(np.float64) - 127.0), 8, axis=1)[..., None]
    return vals.transpose(0, 1, 3, 2).reshape(g * 512, n)


E2M1 = np.array([0.0, 0.5, 1.0, 1.5, 2.0, 3.0, 4.0, 6.0, -0.0, -0.5, -1.0, -1.5, -2.0, -3.0, -4.0, -6.0])


def pack_fp4(w):
    k, n = w.shape
    w = f64(np.asarray(w, np.float32).astype(ml_dtypes.bfloat16)).reshape(k // 32, 32, n)
    amax = np.abs(w).max(1)
    mant, ex = np.frexp(amax / 6.0)
    byte = np.clip(np.where(amax > 0, np.where(mant > 0.5, ex, ex - 1) + 127, 1), 1, 254)
    scaled = (w * np.exp2(127.0 - byte)[:, None, :]).reshape(k, n).astype(np.float32)
    c = np.ascontiguousarray(scaled.reshape(k // 512, 128, 4, n).transpose(0, 1, 3, 2)).astype(ml_dtypes.float4_e2m1fn).view(np.uint8) & 0xF
    words = (c[..., 0::2] | (c[..., 1::2] << 4)).reshape(k // 512, 128, 2 * n)
    return np.ascontiguousarray(words), np.ascontiguousarray(byte.astype(np.uint8).reshape(k // 512, 16, n))


def unpack_fp4(words, scales):
    g, _, n = scales.shape
    words = np.ascontiguousarray(words).reshape(g, 128, n, 2)
    nib = np.empty((g, 128, n, 4), np.uint8)
    nib[..., 0::2] = words & 0xF
    nib[..., 1::2] = words >> 4
    vals = E2M1[nib] * np.repeat(np.exp2(scales.astype(np.float64) - 127.0), 8, axis=1)[..., None]
    return vals.transpose(0, 1, 3, 2).reshape(g * 512, n)


def planes(y):
    n, m = y.shape
    v = y.astype(np.float32).astype(ml_dtypes.bfloat16).astype(np.float64).reshape(n // 32, 32, m)
    top = np.abs(v).max(1)
    byte = np.clip(np.where(top > 0, np.frexp(top)[1] - 1 + 127 - 7, 1), 1, 254)
    codes = (v * np.exp2(127.0 - byte)[:, None, :]).reshape(n, m).astype(np.float32).astype(ml_dtypes.float8_e4m3fn).view(np.uint8)
    words = codes.reshape(n // 512, 128, 4, m).transpose(0, 1, 3, 2)
    return np.ascontiguousarray(words), np.ascontiguousarray(byte.astype(np.uint8).reshape(n // 512, 16, m))


K, T, S, N, H = 512, 2048, 512, 512, 512


def setup_inputs():
    n = np.random.standard_normal
    s = mx_kscale(K)[:, None]
    u = mx_kscale(H)
    packed_xT = pack_weight(n((K, T)) * s)
    packed_w1 = pack_fp4(n((K, H)) / np.sqrt(K) / s)
    packed_w2 = pack_fp4(n((H, N)) / np.sqrt(H) / u[:, None])
    return {
        "x_words": packed_xT[0],
        "x_scales": packed_xT[1],
        "w1_words": packed_w1[0],
        "w1_scales": packed_w1[1],
        "gn": (np.random.uniform(0.5, 1.5, (H, 1)) * u[:, None]).astype(np.float32),
        "w2_words": packed_w2[0],
        "w2_scales": packed_w2[1],
        "offs": striped8(np.random.randint(0, T, (8, S))),
        "n1": striped8(np.stack([np.random.permutation(S) for _ in range(8)])),
        "n2": striped8(np.stack([np.random.permutation(S) for _ in range(8)])),
    }


def reference(x_words, x_scales, w1_words, w1_scales, gn, w2_words, w2_scales, offs, n1, n2):
    xq = unpack_weight(x_words, x_scales)[np.arange(K)[:, None], runs(offs, K)]
    y = unpack_fp4(w1_words, w1_scales).T @ xq
    p = (y[np.arange(H)[:, None], runs(n1, H)]) * (y[np.arange(H)[:, None], runs(n2, H)])
    z = f64(gn) * (p[np.arange(H)[:, None], runs(n1, H)] - (0.5 * p))
    out_0 = unpack_fp4(w2_words, w2_scales).T @ mxq(z, 0, "e4m3")
    return (out_0,) + planes(out_0)

@@ -1,0 +1,202 @@
+from contextlib import ExitStack
+
+import concourse.mybir as mybir
+
+F32 = mybir.dt.float32
+BF16 = mybir.dt.bfloat16
+I32 = mybir.dt.int32
+U32 = mybir.dt.uint32
+U16 = mybir.dt.uint16
+U8 = mybir.dt.uint8
+FP8X4 = mybir.dt.float8_e4m3fn_x4
+FP4X4 = mybir.dt.float4_e2m1fn_x4
+COPY = mybir.ActivationFunctionType.Copy
+MULT = mybir.AluOpType.mult
+SUBTRACT = mybir.AluOpType.subtract
+
+P = 128
+PACK = 4
+T = 2048
+S = 512
+HALF = S // 2
+CHUNK = 128
+CHUNKS = S // CHUNK
+FLOPS = 2 * 2 * 512 * 512 * 512
+
+
+def tile_picked_hashprod_none_po_kernel(
+    tc, x_words, x_scales, w1_words, w1_scales, gn, w2_words, w2_scales, offs, n1, n2, out_0, out_1, out_2
+):
+    nc = tc.nc
+    with ExitStack() as ctx:
+        sb = ctx.enter_context(tc.tile_pool(name="sb", bufs=1))
+        ps = ctx.enter_context(tc.psum_pool(name="ps", bufs=1))
+
+        def tile(shape, dtype, name, tag=None):
+            return sb.tile(shape, dtype, name=name, tag=tag or name, align_bytes=64)
+
+        offs_sb = tile([P, S // 16], U16, "offs_sb")
+        n1_sb = tile([P, S // 16], U16, "n1_sb")
+        n2_sb = tile([P, S // 16], U16, "n2_sb")
+        table_words = tile([P, T], U32, "table_words")
+        table_scales = tile([P, T], U8, "table_scales")
+        picked_words = tile([P, S], U32, "picked_words")
+        picked_scales = tile([P, S], U8, "picked_scales")
+        placed_scales = tile([P, S], U8, "placed_scales")
+        raw_words = [tile([P, 2 * S], U8, "raw_words0")]
+        raw_scales = [tile([P, S], U8, f"raw_scales{w}") for w in range(2)]
+        w_words = [tile([P, 2 * S], U8, f"w_words{w}") for w in range(2)]
+        w_scales = [tile([P, S], U8, f"w_scales{w}") for w in range(2)]
+        half_gain = tile([P, PACK], F32, "half_gain")
+        gained = [tile([P, S], F32, f"gained{t}") for t in range(PACK)]
+        plain = [tile([P, 2 * S], F32, f"plain{i}") for i in range(2)]
+        first = [tile([P, S], F32, f"first{i}") for i in range(2)]
+        prod = [tile([P, S], F32, f"prod{t}") for t in range(PACK)]
+        half_prod = [tile([P, S], F32, f"half_prod{t}") for t in range(PACK)]
+        z = [tile([P, PACK, CHUNK], F32, f"z{c}") for c in range(CHUNKS)]
+        z_bf = [tile([P, CHUNK * PACK], BF16, f"z_bf{c}") for c in range(CHUNKS)]
+        z_words = [tile([P, CHUNK], U32, f"z_words{c}") for c in range(CHUNKS)]
+        z_scales = [tile([P, CHUNK], U8, f"z_scales{c}") for c in range(CHUNKS)]
+        res = [tile([P, PACK, CHUNK], F32, f"res{c}") for c in range(CHUNKS)]
+        res_bf = [tile([P, CHUNK * PACK], BF16, f"res_bf{c}") for c in range(CHUNKS)]
+        res_words = tile([P, S], U32, "res_words")
+        res_scales = tile([P, S], U8, "res_scales")
+
+        nc.sync.dma_start(offs_sb[:], offs)
+        nc.scalar.dma_start(raw_words[0][:].bitcast(I32), w1_words[0].bitcast(I32))
+        nc.sync.dma_start(table_words[:].bitcast(I32), x_words[0].rearrange("p n t -> p (n t)").bitcast(I32))
+        nc.vector.memset(table_scales[:].bitcast(I32), 0)
+        nc.scalar.dma_start(table_scales[:].bitcast(I32)[0:P:8, :], x_scales[0].bitcast(I32))
+        nc.gpsimd.memset(raw_scales[0][:].bitcast(I32), 0)
+        for q in range(4):
+            queue = nc.scalar if q < 2 else nc.gpsimd
+            queue.dma_start(
+                raw_scales[0][:].bitcast(I32)[32 * q : 32 * q + 4, :], w1_scales[0].bitcast(I32)[4 * q : 4 * q + 4, :]
+            )
+        nc.sync.dma_start(n1_sb[:], n1)
+        nc.sync.dma_start(n2_sb[:], n2)
+        nc.vector.memset(raw_scales[1][:].bitcast(I32), 0)
+        for q in range(4):
+            nc.sync.dma_start(
+                raw_scales[1][:].bitcast(I32)[32 * q : 32 * q + 4, :], w2_scales[0].bitcast(I32)[4 * q : 4 * q + 4, :]
+            )
+        nc.vector.memset(placed_scales[:].bitcast(I32), 0)
+        nc.vector.memset(plain[0][:, S:], 0.0)
+        nc.scalar.activation(plain[1][:, S:], plain[0][:, S:], COPY)
+
+        def deal(w):
+            nc.vector.tensor_copy(
+                w_words[w][:].rearrange("p (t m b) -> p m t b", t=PACK, b=2),
+                raw_words[w][:].rearrange("p (m t b) -> p m t b", t=PACK, b=2),
+            )
+            nc.vector.tensor_copy(
+                w_scales[w][:].rearrange("p (t m) -> p m t", t=PACK),
+                raw_scales[w][:].rearrange("p (m t) -> p m t", t=PACK),
+            )
+
+        nc.vector.tensor_copy(picked_scales[:], table_scales[:].indirect(offs_sb[:]))
+        for s in range(4):
+            nc.scalar.dma_start(
+                placed_scales[:].bitcast(I32)[s:P:32, :], picked_scales[:].bitcast(I32)[8 * s : P : 32, :]
+            )
+        deal(0)
+        raw_words.append(tile([P, 2 * S], U8, "raw_words1", tag="raw_words0"))
+        nc.sync.dma_start(raw_words[1][:].bitcast(I32), w2_words[0].bitcast(I32))
+        gain = tile([P, PACK], F32, "gain", tag="raw_scales0")
+        nc.sync.dma_start(gain[:], gn.rearrange("(p t) o -> p (t o)", t=PACK))
+
+        def product(bank, w, t, words, scales):
+            nc.tensor.matmul_mx(
+                out=bank,
+                lhsT=w_words[w][:, 2 * P * t : 2 * P * (t + 1)].bitcast(FP4X4),
+                lhsT_scale=w_scales[w][:, P * t : P * (t + 1)],
+                rhs=words.bitcast(FP8X4),
+                rhs_scale=scales,
+                start=True,
+                stop=True,
+            )
+
+        y0 = [ps.tile([P, HALF], F32, name=f"y0_{h}") for h in range(2)]
+        y = [ps.tile([P, S], F32, name=f"y{t}") for t in range(1, PACK)]
+        for h in range(2):
+            cols = slice(h * HALF, (h + 1) * HALF)
+            nc.vector.tensor_copy(
+                picked_words[:, cols], table_words[:].indirect(offs_sb[:, h * HALF // 16 : (h + 1) * HALF // 16])
+            )
+            product(y0[h][:], 0, 0, picked_words[:, cols], placed_scales[:, cols])
+        for t in range(1, PACK):
+            product(y[t - 1][:], 0, t, picked_words[:], placed_scales[:])
+        deal(1)
+
+        def y_parts(t):
+            if t == 0:
+                return [(slice(h * HALF, (h + 1) * HALF), y0[h][:]) for h in range(2)]
+            return [(slice(0, S), y[t - 1][:])]
+
+        def evac_plain(t):
+            for cols, bank in y_parts(t):
+                nc.scalar.activation(plain[t % 2][:, cols], bank, COPY)
+
+        nc.scalar.activation(half_gain[:], gain[:], COPY, scale=0.5)
+        for pair in ((0, 1), (2, 3)):
+            for t in pair:
+                evac_plain(t)
+            for t in pair:
+                nc.vector.tensor_copy(first[t % 2][:], plain[t % 2][:].indirect(n1_sb[:]))
+            for t in pair:
+                nc.vector.tensor_tensor(prod[t][:], plain[t % 2][:].indirect(n2_sb[:]), first[t % 2][:], MULT)
+        for t in range(PACK):
+            nc.scalar.activation(gained[t][:], prod[t][:], COPY, scale=gain[:, t : t + 1])
+            nc.scalar.activation(half_prod[t][:], prod[t][:], COPY, scale=half_gain[:, t : t + 1])
+
+        def interleave(copy, dst, src):
+            copy(
+                dst[:].rearrange("p (c i t) -> p c t i", i=4, t=PACK),
+                src[:].rearrange("p t (c i) -> p c t i", i=4),
+            )
+
+        banks = [ps.tile([P, PACK, CHUNK], F32, name=f"o{i}") for i in range(3)]
+        out_rows = out_0.rearrange("(p t) j -> p t j", t=PACK)
+        out_words = out_1[0].rearrange("p n t -> p (n t)").bitcast(I32)
+
+        def fetch_z(c):
+            cols = slice(c * CHUNK, (c + 1) * CHUNK)
+            for t in range(PACK):
+                nc.vector.tensor_tensor(
+                    z[c][:, t, :],
+                    gained[t][:].indirect(n1_sb[:, c * CHUNK // 16 : (c + 1) * CHUNK // 16]),
+                    half_prod[t][:, cols],
+                    SUBTRACT,
+                )
+
+        def round_z(c):
+            interleave(nc.vector.tensor_copy if c == CHUNKS - 1 else nc.scalar.copy, z_bf[c], z[c])
+
+        def second_layer(c):
+            cols = slice(c * CHUNK, (c + 1) * CHUNK)
+            nc.vector.quantize_mx(z_words[c][:].bitcast(FP8X4), z_scales[c][:], z_bf[c][:])
+            for t in range(PACK):
+                product(banks[c % 3][:, t, :], 1, t, z_words[c][:], z_scales[c][:])
+            nc.scalar.activation(res[c][:], banks[c % 3][:], COPY)
+            nc.sync.dma_start(out_rows[:, :, cols], res[c][:])
+
+        def planes(c):
+            cols = slice(c * CHUNK, (c + 1) * CHUNK)
+            interleave(nc.vector.tensor_copy, res_bf[c], res[c])
+            nc.vector.quantize_mx(res_words[:, cols].bitcast(FP8X4), res_scales[:, cols], res_bf[c][:])
+            nc.sync.dma_start(out_words[:, cols], res_words[:, cols].bitcast(I32))
+
+        fetch_z(0)
+        round_z(0)
+        for c in range(1, CHUNKS):
+            fetch_z(c)
+            round_z(c)
+            second_layer(c - 1)
+        second_layer(CHUNKS - 1)
+        for c in range(CHUNKS):
+            planes(c)
+        for q in range(4):
+            queue = nc.scalar if q % 2 else nc.sync
+            queue.dma_start(
+                out_2[0].bitcast(I32)[4 * q : 4 * q + 4, :], res_scales[:].bitcast(I32)[32 * q : 32 * q + 4, :]
+            )

@@ -19,8 +19,8 @@ PACK = 4
 T = 2048
 S = 512
 HALF = S // 2
-CHUNK = 128
-CHUNKS = S // CHUNK
+CHUNKS = (slice(0, 256), slice(256, 384), slice(384, 512))
+LAST = len(CHUNKS) - 1
 FLOPS = 2 * 2 * 512 * 512 * 512
 
 
@@ -44,7 +44,7 @@ def tile_picked_hashprod_none_po_kernel(
         picked_scales = tile([P, S], U8, "picked_scales")
         placed_scales = tile([P, S], U8, "placed_scales")
         raw_words = [tile([P, 2 * S], U8, "raw_words0")]
-        raw_scales = [tile([P, S], U8, f"raw_scales{w}") for w in range(2)]
+        raw_scales = tile([P, S], U8, "raw_scales")
         w_words = [tile([P, 2 * S], U8, f"w_words{w}") for w in range(2)]
         w_scales = [tile([P, S], U8, f"w_scales{w}") for w in range(2)]
         half_gain = tile([P, PACK], F32, "half_gain")
@@ -53,57 +53,51 @@ def tile_picked_hashprod_none_po_kernel(
         first = [tile([P, S], F32, f"first{i}") for i in range(2)]
         prod = [tile([P, S], F32, f"prod{t}") for t in range(PACK)]
         half_prod = [tile([P, S], F32, f"half_prod{t}") for t in range(PACK)]
-        z = [tile([P, PACK, CHUNK], F32, f"z{c}") for c in range(CHUNKS)]
-        z_bf = [tile([P, CHUNK * PACK], BF16, f"z_bf{c}") for c in range(CHUNKS)]
-        z_words = [tile([P, CHUNK], U32, f"z_words{c}") for c in range(CHUNKS)]
-        z_scales = [tile([P, CHUNK], U8, f"z_scales{c}") for c in range(CHUNKS)]
-        res = [tile([P, PACK, CHUNK], F32, f"res{c}") for c in range(CHUNKS)]
-        res_bf = [tile([P, CHUNK * PACK], BF16, f"res_bf{c}") for c in range(CHUNKS)]
         res_words = tile([P, S], U32, "res_words")
         res_scales = tile([P, S], U8, "res_scales")
 
-        nc.sync.dma_start(offs_sb[:], offs)
-        nc.scalar.dma_start(raw_words[0][:].bitcast(I32), w1_words[0].bitcast(I32))
-        nc.sync.dma_start(table_words[:].bitcast(I32), x_words[0].rearrange("p n t -> p (n t)").bitcast(I32))
+        def load_scale_rows(w, rows, queue):
+            for q in range(4):
+                queue.dma_start(
+                    raw_scales[:].bitcast(I32)[32 * q : 32 * q + 4, :], rows[0].bitcast(I32)[4 * q : 4 * q + 4, :]
+                )
+
         nc.vector.memset(table_scales[:].bitcast(I32), 0)
-        nc.scalar.dma_start(table_scales[:].bitcast(I32)[0:P:8, :], x_scales[0].bitcast(I32))
-        nc.gpsimd.memset(raw_scales[0][:].bitcast(I32), 0)
-        for q in range(4):
-            queue = nc.scalar if q < 2 else nc.gpsimd
-            queue.dma_start(
-                raw_scales[0][:].bitcast(I32)[32 * q : 32 * q + 4, :], w1_scales[0].bitcast(I32)[4 * q : 4 * q + 4, :]
-            )
+        nc.gpsimd.memset(raw_scales[:].bitcast(I32), 0)
+        nc.sync.dma_start(offs_sb[:], offs)
+        nc.sync.dma_start(table_scales[:].bitcast(I32)[0:P:8, :], x_scales[0].bitcast(I32))
+        nc.sync.dma_start(raw_words[0][:].bitcast(I32), w1_words[0].bitcast(I32))
+        load_scale_rows(0, w1_scales, nc.scalar)
+        nc.sync.dma_start(table_words[:].bitcast(I32), x_words[0].rearrange("p n t -> p (n t)").bitcast(I32))
         nc.sync.dma_start(n1_sb[:], n1)
         nc.sync.dma_start(n2_sb[:], n2)
-        nc.vector.memset(raw_scales[1][:].bitcast(I32), 0)
-        for q in range(4):
-            nc.sync.dma_start(
-                raw_scales[1][:].bitcast(I32)[32 * q : 32 * q + 4, :], w2_scales[0].bitcast(I32)[4 * q : 4 * q + 4, :]
-            )
-        nc.vector.memset(placed_scales[:].bitcast(I32), 0)
         nc.vector.memset(plain[0][:, S:], 0.0)
         nc.scalar.activation(plain[1][:, S:], plain[0][:, S:], COPY)
 
-        def deal(w):
-            nc.vector.tensor_copy(
-                w_words[w][:].rearrange("p (t m b) -> p m t b", t=PACK, b=2),
-                raw_words[w][:].rearrange("p (m t b) -> p m t b", t=PACK, b=2),
+        def deal_words(w):
+            nc.gpsimd.tensor_copy(
+                w_words[w][:].rearrange("p (t m b) -> p t m b", t=PACK, b=2),
+                raw_words[w][:].rearrange("p (m t b) -> p t m b", t=PACK, b=2),
             )
-            nc.vector.tensor_copy(
-                w_scales[w][:].rearrange("p (t m) -> p m t", t=PACK),
-                raw_scales[w][:].rearrange("p (m t) -> p m t", t=PACK),
+
+        def deal_scales(w):
+            nc.gpsimd.tensor_copy(
+                w_scales[w][:].rearrange("p (t m) -> p t m", t=PACK),
+                raw_scales[:].rearrange("p (m t) -> p t m", t=PACK),
             )
 
         nc.vector.tensor_copy(picked_scales[:], table_scales[:].indirect(offs_sb[:]))
-        for s in range(4):
-            nc.scalar.dma_start(
+        nc.vector.tensor_copy(placed_scales[:].bitcast(I32), picked_scales[:].bitcast(I32))
+        for s in range(1, 4):
+            queue = nc.scalar if s % 2 else nc.sync
+            queue.dma_start(
                 placed_scales[:].bitcast(I32)[s:P:32, :], picked_scales[:].bitcast(I32)[8 * s : P : 32, :]
             )
-        deal(0)
-        raw_words.append(tile([P, 2 * S], U8, "raw_words1", tag="raw_words0"))
+        deal_words(0)
+        deal_scales(0)
+        load_scale_rows(1, w2_scales, nc.sync)
+        raw_words.append(tile([P, 2 * S], U8, "raw_words1", tag="picked_scales"))
         nc.sync.dma_start(raw_words[1][:].bitcast(I32), w2_words[0].bitcast(I32))
-        gain = tile([P, PACK], F32, "gain", tag="raw_scales0")
-        nc.sync.dma_start(gain[:], gn.rearrange("(p t) o -> p (t o)", t=PACK))
 
         def product(bank, w, t, words, scales):
             nc.tensor.matmul_mx(
@@ -126,7 +120,10 @@ def tile_picked_hashprod_none_po_kernel(
             product(y0[h][:], 0, 0, picked_words[:, cols], placed_scales[:, cols])
         for t in range(1, PACK):
             product(y[t - 1][:], 0, t, picked_words[:], placed_scales[:])
-        deal(1)
+        gain = tile([P, PACK], F32, "gain", tag="table_words")
+        nc.sync.dma_start(gain[:], gn.rearrange("(p t) o -> p (t o)", t=PACK))
+        deal_words(1)
+        deal_scales(1)
 
         def y_parts(t):
             if t == 0:
@@ -135,7 +132,10 @@ def tile_picked_hashprod_none_po_kernel(
 
         def evac_plain(t):
             for cols, bank in y_parts(t):
-                nc.scalar.activation(plain[t % 2][:, cols], bank, COPY)
+                if cols.start == 0:
+                    nc.scalar.activation(plain[t % 2][:, cols], bank, COPY)
+                else:
+                    nc.vector.tensor_copy(plain[t % 2][:, cols], bank)
 
         nc.scalar.activation(half_gain[:], gain[:], COPY, scale=0.5)
         for pair in ((0, 1), (2, 3)):
@@ -151,50 +151,74 @@ def tile_picked_hashprod_none_po_kernel(
 
         def interleave(copy, dst, src):
             copy(
-                dst[:].rearrange("p (c i t) -> p c t i", i=4, t=PACK),
-                src[:].rearrange("p t (c i) -> p c t i", i=4),
+                dst.rearrange("p (c i t) -> p c t i", i=4, t=PACK),
+                src.rearrange("p (t c i) -> p c t i", i=4, t=PACK),
             )
 
-        banks = [ps.tile([P, PACK, CHUNK], F32, name=f"o{i}") for i in range(3)]
+        def width(c):
+            return CHUNKS[c].stop - CHUNKS[c].start
+
         out_rows = out_0.rearrange("(p t) j -> p t j", t=PACK)
         out_words = out_1[0].rearrange("p n t -> p (n t)").bitcast(I32)
+        z, z_bf, res = {}, {}, {}
 
-        def fetch_z(c):
-            cols = slice(c * CHUNK, (c + 1) * CHUNK)
-            for t in range(PACK):
-                nc.vector.tensor_tensor(
-                    z[c][:, t, :],
-                    gained[t][:].indirect(n1_sb[:, c * CHUNK // 16 : (c + 1) * CHUNK // 16]),
-                    half_prod[t][:, cols],
-                    SUBTRACT,
-                )
+        def fetch_z(c, t):
+            cols, n = CHUNKS[c], width(c)
+            nc.vector.tensor_tensor(
+                z[c][:, t * n : (t + 1) * n],
+                gained[t][:].indirect(n1_sb[:, cols.start // 16 : cols.stop // 16]),
+                half_prod[t][:, cols],
+                SUBTRACT,
+            )
 
-        def round_z(c):
-            interleave(nc.vector.tensor_copy if c == CHUNKS - 1 else nc.scalar.copy, z_bf[c], z[c])
+        def second_layer(c, bank_tags):
+            cols, n = CHUNKS[c], width(c)
+            z_words = tile([P, n], U32, f"z_words{c}")
+            z_scales = tile([P, n], U8, f"z_scales{c}")
+            nc.vector.quantize_mx(z_words[:].bitcast(FP8X4), z_scales[:], z_bf[c])
+            res[c] = tile([P, PACK * n], F32, f"res{c}")
+            per_bank = PACK // len(bank_tags)
+            for b, tag in enumerate(bank_tags):
+                bank = ps.tile([P, per_bank * n], F32, name=f"o{c}_{b}", tag=tag)
+                for i in range(per_bank):
+                    product(bank[:, i * n : (i + 1) * n], 1, b * per_bank + i, z_words[:], z_scales[:])
+                part = res[c][:, b * per_bank * n : (b + 1) * per_bank * n]
+                if c == LAST and b == len(bank_tags) - 1:
+                    nc.vector.tensor_copy(part, bank[:])
+                else:
+                    nc.scalar.activation(part, bank[:], COPY)
+            nc.sync.dma_start(out_rows[:, :, cols], res[c][:].rearrange("p (t j) -> p t j", t=PACK))
 
-        def second_layer(c):
-            cols = slice(c * CHUNK, (c + 1) * CHUNK)
-            nc.vector.quantize_mx(z_words[c][:].bitcast(FP8X4), z_scales[c][:], z_bf[c][:])
-            for t in range(PACK):
-                product(banks[c % 3][:, t, :], 1, t, z_words[c][:], z_scales[c][:])
-            nc.scalar.activation(res[c][:], banks[c % 3][:], COPY)
-            nc.sync.dma_start(out_rows[:, :, cols], res[c][:])
-
-        def planes(c):
-            cols = slice(c * CHUNK, (c + 1) * CHUNK)
-            interleave(nc.vector.tensor_copy, res_bf[c], res[c])
-            nc.vector.quantize_mx(res_words[:, cols].bitcast(FP8X4), res_scales[:, cols], res_bf[c][:])
+        def planes(c, tag):
+            cols, n = CHUNKS[c], width(c)
+            res_bf = tile([P, PACK * n], BF16, f"res_bf{c}", tag=tag)
+            interleave(nc.vector.tensor_copy, res_bf[:], res[c][:])
+            nc.vector.quantize_mx(res_words[:, cols].bitcast(FP8X4), res_scales[:, cols], res_bf[:])
             nc.sync.dma_start(out_words[:, cols], res_words[:, cols].bitcast(I32))
 
-        fetch_z(0)
-        round_z(0)
-        for c in range(1, CHUNKS):
-            fetch_z(c)
-            round_z(c)
-            second_layer(c - 1)
-        second_layer(CHUNKS - 1)
-        for c in range(CHUNKS):
-            planes(c)
+        for c in range(LAST):
+            z[c] = tile([P, PACK * width(c)], F32, f"z{c}")[:, :]
+            for t in range(PACK):
+                fetch_z(c, t)
+            if c == 0:
+                z_bf[0] = tile([P, PACK * width(0)], BF16, "z_bf0")[:]
+                interleave(nc.scalar.copy, z_bf[0], z[0])
+        second_layer(0, ["o0", "o1"])
+        n = width(LAST)
+        shared = tile([P, (PACK + 1) * n], F32, "shared", tag="z_bf0")
+        z[LAST] = shared[:, : PACK * n]
+        z_bf[1] = shared[:, (PACK - 1) * n :].bitcast(BF16)
+        interleave(nc.scalar.copy, z_bf[1], z[1])
+        for t in range(PACK - 1):
+            fetch_z(LAST, t)
+        second_layer(1, ["o2"])
+        fetch_z(LAST, PACK - 1)
+        z_bf[LAST] = tile([P, PACK * n], BF16, "z_bf2")[:]
+        interleave(nc.vector.tensor_copy, z_bf[LAST], z[LAST])
+        second_layer(LAST, ["y0_0", "y1", "y2", "y3"])
+        planes(0, "z_bf2")
+        planes(1, "z_bf0")
+        planes(LAST, "z1")
         for q in range(4):
             queue = nc.scalar if q % 2 else nc.sync
             queue.dma_start(

@@ -43,9 +43,9 @@ def tile_picked_hashprod_none_po_kernel(
         picked_words = tile([P, S], U32, "picked_words")
         picked_scales = tile([P, S], U8, "picked_scales")
         placed_scales = tile([P, S], U8, "placed_scales")
-        raw_words = [tile([P, 2 * S], U8, "raw_words0")]
+        raw_words = [tile([P, 2 * S], U8, f"raw_words{w}") for w in range(2)]
         raw_scales = tile([P, S], U8, "raw_scales")
-        w_words = [tile([P, 2 * S], U8, f"w_words{w}") for w in range(2)]
+        w_words = []
         w_scales = [tile([P, S], U8, f"w_scales{w}") for w in range(2)]
         half_gain = tile([P, PACK], F32, "half_gain")
         gained = [tile([P, S], F32, f"gained{t}") for t in range(PACK)]
@@ -71,19 +71,22 @@ def tile_picked_hashprod_none_po_kernel(
         nc.sync.dma_start(table_words[:].bitcast(I32), x_words[0].rearrange("p n t -> p (n t)").bitcast(I32))
         nc.sync.dma_start(n1_sb[:], n1)
         nc.sync.dma_start(n2_sb[:], n2)
+        nc.sync.dma_start(raw_words[1][:].bitcast(I32), w2_words[0].bitcast(I32))
         nc.vector.memset(plain[0][:, S:], 0.0)
         nc.scalar.activation(plain[1][:, S:], plain[0][:, S:], COPY)
 
-        def deal_words(w):
-            nc.gpsimd.tensor_copy(
-                w_words[w][:].rearrange("p (t m b) -> p t m b", t=PACK, b=2),
-                raw_words[w][:].rearrange("p (m t b) -> p t m b", t=PACK, b=2),
+        def deal_words(w, tag):
+            w_words.append(tile([P, 2 * S], U8, f"w_words{w}", tag=tag))
+            nc.vector.tensor_copy(
+                w_words[w][:].rearrange("p (t m b) -> p m t b", t=PACK, b=2),
+                raw_words[w][:].rearrange("p (m t b) -> p m t b", t=PACK, b=2),
             )
 
         def deal_scales(w):
-            nc.gpsimd.tensor_copy(
-                w_scales[w][:].rearrange("p (t m) -> p t m", t=PACK),
-                raw_scales[:].rearrange("p (m t) -> p t m", t=PACK),
+            order = "p t m" if w else "p m t"
+            (nc.gpsimd if w else nc.vector).tensor_copy(
+                w_scales[w][:].rearrange("p (t m) -> " + order, t=PACK),
+                raw_scales[:].rearrange("p (m t) -> " + order, t=PACK),
             )
 
         nc.vector.tensor_copy(picked_scales[:], table_scales[:].indirect(offs_sb[:]))
@@ -93,11 +96,11 @@ def tile_picked_hashprod_none_po_kernel(
             queue.dma_start(
                 placed_scales[:].bitcast(I32)[s:P:32, :], picked_scales[:].bitcast(I32)[8 * s : P : 32, :]
             )
-        deal_words(0)
+        deal_words(0, "table_scales")
         deal_scales(0)
         load_scale_rows(1, w2_scales, nc.sync)
-        raw_words.append(tile([P, 2 * S], U8, "raw_words1", tag="picked_scales"))
-        nc.sync.dma_start(raw_words[1][:].bitcast(I32), w2_words[0].bitcast(I32))
+        gain = tile([P, PACK], F32, "gain", tag="picked_scales")
+        nc.sync.dma_start(gain[:], gn.rearrange("(p t) o -> p (t o)", t=PACK))
 
         def product(bank, w, t, words, scales):
             nc.tensor.matmul_mx(
@@ -120,9 +123,7 @@ def tile_picked_hashprod_none_po_kernel(
             product(y0[h][:], 0, 0, picked_words[:, cols], placed_scales[:, cols])
         for t in range(1, PACK):
             product(y[t - 1][:], 0, t, picked_words[:], placed_scales[:])
-        gain = tile([P, PACK], F32, "gain", tag="table_words")
-        nc.sync.dma_start(gain[:], gn.rearrange("(p t) o -> p (t o)", t=PACK))
-        deal_words(1)
+        deal_words(1, "table_words")
         deal_scales(1)
 
         def y_parts(t):
@@ -183,10 +184,7 @@ def tile_picked_hashprod_none_po_kernel(
                 for i in range(per_bank):
                     product(bank[:, i * n : (i + 1) * n], 1, b * per_bank + i, z_words[:], z_scales[:])
                 part = res[c][:, b * per_bank * n : (b + 1) * per_bank * n]
-                if c == LAST and b == len(bank_tags) - 1:
-                    nc.vector.tensor_copy(part, bank[:])
-                else:
-                    nc.scalar.activation(part, bank[:], COPY)
+                nc.scalar.activation(part, bank[:], COPY)
             nc.sync.dma_start(out_rows[:, :, cols], res[c][:].rearrange("p (t j) -> p t j", t=PACK))
 
         def planes(c, tag):

from contextlib import ExitStack

import concourse.mybir as mybir

F32 = mybir.dt.float32
BF16 = mybir.dt.bfloat16
I32 = mybir.dt.int32
U32 = mybir.dt.uint32
U16 = mybir.dt.uint16
U8 = mybir.dt.uint8
FP8X4 = mybir.dt.float8_e4m3fn_x4
FP4X4 = mybir.dt.float4_e2m1fn_x4
COPY = mybir.ActivationFunctionType.Copy
MULT = mybir.AluOpType.mult
SUBTRACT = mybir.AluOpType.subtract

P = 128
PACK = 4
T = 2048
S = 512
HALF = S // 2
CHUNKS = (slice(0, 256), slice(256, 384), slice(384, 512))
LAST = len(CHUNKS) - 1
FLOPS = 2 * 2 * 512 * 512 * 512


def tile_picked_hashprod_none_po_kernel(
    tc, x_words, x_scales, w1_words, w1_scales, gn, w2_words, w2_scales, offs, n1, n2, out_0, out_1, out_2
):
    nc = tc.nc
    with ExitStack() as ctx:
        sb = ctx.enter_context(tc.tile_pool(name="sb", bufs=1))
        ps = ctx.enter_context(tc.psum_pool(name="ps", bufs=1))

        def tile(shape, dtype, name, tag=None):
            return sb.tile(shape, dtype, name=name, tag=tag or name, align_bytes=64)

        offs_sb = tile([P, S // 16], U16, "offs_sb")
        n1_sb = tile([P, S // 16], U16, "n1_sb")
        n2_sb = tile([P, S // 16], U16, "n2_sb")
        table_words = tile([P, T], U32, "table_words")
        table_scales = tile([P, T], U8, "table_scales")
        picked_words = tile([P, S], U32, "picked_words")
        picked_scales = tile([P, S], U8, "picked_scales")
        placed_scales = tile([P, S], U8, "placed_scales")
        raw_words = [tile([P, 2 * S], U8, f"raw_words{w}") for w in range(2)]
        raw_scales = tile([P, S], U8, "raw_scales")
        w_words = []
        w_scales = [tile([P, S], U8, f"w_scales{w}") for w in range(2)]
        half_gain = tile([P, PACK], F32, "half_gain")
        gained = [tile([P, S], F32, f"gained{t}") for t in range(PACK)]
        plain = [tile([P, 2 * S], F32, f"plain{i}") for i in range(2)]
        first = [tile([P, S], F32, f"first{i}") for i in range(2)]
        prod = [tile([P, S], F32, f"prod{t}") for t in range(PACK)]
        half_prod = [tile([P, S], F32, f"half_prod{t}") for t in range(PACK)]
        res_words = tile([P, S], U32, "res_words")
        res_scales = tile([P, S], U8, "res_scales")

        def load_scale_rows(w, rows, queue):
            for q in range(4):
                queue.dma_start(
                    raw_scales[:].bitcast(I32)[32 * q : 32 * q + 4, :], rows[0].bitcast(I32)[4 * q : 4 * q + 4, :]
                )

        nc.vector.memset(table_scales[:].bitcast(I32), 0)
        nc.gpsimd.memset(raw_scales[:].bitcast(I32), 0)
        nc.sync.dma_start(offs_sb[:], offs)
        nc.sync.dma_start(table_scales[:].bitcast(I32)[0:P:8, :], x_scales[0].bitcast(I32))
        nc.sync.dma_start(raw_words[0][:].bitcast(I32), w1_words[0].bitcast(I32))
        load_scale_rows(0, w1_scales, nc.scalar)
        nc.sync.dma_start(table_words[:].bitcast(I32), x_words[0].rearrange("p n t -> p (n t)").bitcast(I32))
        nc.sync.dma_start(n1_sb[:], n1)
        nc.sync.dma_start(n2_sb[:], n2)
        nc.sync.dma_start(raw_words[1][:].bitcast(I32), w2_words[0].bitcast(I32))
        nc.vector.memset(plain[0][:, S:], 0.0)
        nc.scalar.activation(plain[1][:, S:], plain[0][:, S:], COPY)

        def deal_words(w, tag):
            w_words.append(tile([P, 2 * S], U8, f"w_words{w}", tag=tag))
            nc.vector.tensor_copy(
                w_words[w][:].rearrange("p (t m b) -> p m t b", t=PACK, b=2),
                raw_words[w][:].rearrange("p (m t b) -> p m t b", t=PACK, b=2),
            )

        def deal_scales(w):
            order = "p t m" if w else "p m t"
            (nc.gpsimd if w else nc.vector).tensor_copy(
                w_scales[w][:].rearrange("p (t m) -> " + order, t=PACK),
                raw_scales[:].rearrange("p (m t) -> " + order, t=PACK),
            )

        nc.vector.tensor_copy(picked_scales[:], table_scales[:].indirect(offs_sb[:]))
        nc.vector.tensor_copy(placed_scales[:].bitcast(I32), picked_scales[:].bitcast(I32))
        for s in range(1, 4):
            queue = nc.scalar if s % 2 else nc.sync
            queue.dma_start(
                placed_scales[:].bitcast(I32)[s:P:32, :], picked_scales[:].bitcast(I32)[8 * s : P : 32, :]
            )
        deal_words(0, "table_scales")
        deal_scales(0)
        load_scale_rows(1, w2_scales, nc.sync)
        gain = tile([P, PACK], F32, "gain", tag="picked_scales")
        nc.sync.dma_start(gain[:], gn.rearrange("(p t) o -> p (t o)", t=PACK))

        def product(bank, w, t, words, scales):
            nc.tensor.matmul_mx(
                out=bank,
                lhsT=w_words[w][:, 2 * P * t : 2 * P * (t + 1)].bitcast(FP4X4),
                lhsT_scale=w_scales[w][:, P * t : P * (t + 1)],
                rhs=words.bitcast(FP8X4),
                rhs_scale=scales,
                start=True,
                stop=True,
            )

        y0 = [ps.tile([P, HALF], F32, name=f"y0_{h}") for h in range(2)]
        y = [ps.tile([P, S], F32, name=f"y{t}") for t in range(1, PACK)]
        for h in range(2):
            cols = slice(h * HALF, (h + 1) * HALF)
            nc.vector.tensor_copy(
                picked_words[:, cols], table_words[:].indirect(offs_sb[:, h * HALF // 16 : (h + 1) * HALF // 16])
            )
            product(y0[h][:], 0, 0, picked_words[:, cols], placed_scales[:, cols])
        for t in range(1, PACK):
            product(y[t - 1][:], 0, t, picked_words[:], placed_scales[:])
        deal_words(1, "table_words")
        deal_scales(1)

        def y_parts(t):
            if t == 0:
                return [(slice(h * HALF, (h + 1) * HALF), y0[h][:]) for h in range(2)]
            return [(slice(0, S), y[t - 1][:])]

        def evac_plain(t):
            for cols, bank in y_parts(t):
                if cols.start == 0:
                    nc.scalar.activation(plain[t % 2][:, cols], bank, COPY)
                else:
                    nc.vector.tensor_copy(plain[t % 2][:, cols], bank)

        nc.scalar.activation(half_gain[:], gain[:], COPY, scale=0.5)
        for pair in ((0, 1), (2, 3)):
            for t in pair:
                evac_plain(t)
            for t in pair:
                nc.vector.tensor_copy(first[t % 2][:], plain[t % 2][:].indirect(n1_sb[:]))
            for t in pair:
                nc.vector.tensor_tensor(prod[t][:], plain[t % 2][:].indirect(n2_sb[:]), first[t % 2][:], MULT)
        for t in range(PACK):
            nc.scalar.activation(gained[t][:], prod[t][:], COPY, scale=gain[:, t : t + 1])
            nc.scalar.activation(half_prod[t][:], prod[t][:], COPY, scale=half_gain[:, t : t + 1])

        def interleave(copy, dst, src):
            copy(
                dst.rearrange("p (c i t) -> p c t i", i=4, t=PACK),
                src.rearrange("p (t c i) -> p c t i", i=4, t=PACK),
            )

        def width(c):
            return CHUNKS[c].stop - CHUNKS[c].start

        out_rows = out_0.rearrange("(p t) j -> p t j", t=PACK)
        out_words = out_1[0].rearrange("p n t -> p (n t)").bitcast(I32)
        z, z_bf, res = {}, {}, {}

        def fetch_z(c, t):
            cols, n = CHUNKS[c], width(c)
            nc.vector.tensor_tensor(
                z[c][:, t * n : (t + 1) * n],
                gained[t][:].indirect(n1_sb[:, cols.start // 16 : cols.stop // 16]),
                half_prod[t][:, cols],
                SUBTRACT,
            )

        def second_layer(c, bank_tags):
            cols, n = CHUNKS[c], width(c)
            z_words = tile([P, n], U32, f"z_words{c}")
            z_scales = tile([P, n], U8, f"z_scales{c}")
            nc.vector.quantize_mx(z_words[:].bitcast(FP8X4), z_scales[:], z_bf[c])
            res[c] = tile([P, PACK * n], F32, f"res{c}")
            per_bank = PACK // len(bank_tags)
            for b, tag in enumerate(bank_tags):
                bank = ps.tile([P, per_bank * n], F32, name=f"o{c}_{b}", tag=tag)
                for i in range(per_bank):
                    product(bank[:, i * n : (i + 1) * n], 1, b * per_bank + i, z_words[:], z_scales[:])
                part = res[c][:, b * per_bank * n : (b + 1) * per_bank * n]
                nc.scalar.activation(part, bank[:], COPY)
            nc.sync.dma_start(out_rows[:, :, cols], res[c][:].rearrange("p (t j) -> p t j", t=PACK))

        def planes(c, tag):
            cols, n = CHUNKS[c], width(c)
            res_bf = tile([P, PACK * n], BF16, f"res_bf{c}", tag=tag)
            interleave(nc.vector.tensor_copy, res_bf[:], res[c][:])
            nc.vector.quantize_mx(res_words[:, cols].bitcast(FP8X4), res_scales[:, cols], res_bf[:])
            nc.sync.dma_start(out_words[:, cols], res_words[:, cols].bitcast(I32))

        for c in range(LAST):
            z[c] = tile([P, PACK * width(c)], F32, f"z{c}")[:, :]
            for t in range(PACK):
                fetch_z(c, t)
            if c == 0:
                z_bf[0] = tile([P, PACK * width(0)], BF16, "z_bf0")[:]
                interleave(nc.scalar.copy, z_bf[0], z[0])
        second_layer(0, ["o0", "o1"])
        n = width(LAST)
        shared = tile([P, (PACK + 1) * n], F32, "shared", tag="z_bf0")
        z[LAST] = shared[:, : PACK * n]
        z_bf[1] = shared[:, (PACK - 1) * n :].bitcast(BF16)
        interleave(nc.scalar.copy, z_bf[1], z[1])
        for t in range(PACK - 1):
            fetch_z(LAST, t)
        second_layer(1, ["o2"])
        fetch_z(LAST, PACK - 1)
        z_bf[LAST] = tile([P, PACK * n], BF16, "z_bf2")[:]
        interleave(nc.vector.tensor_copy, z_bf[LAST], z[LAST])
        second_layer(LAST, ["y0_0", "y1", "y2", "y3"])
        planes(0, "z_bf2")
        planes(1, "z_bf0")
        planes(LAST, "z1")
        for q in range(4):
            queue = nc.scalar if q % 2 else nc.sync
            queue.dma_start(
                out_2[0].bitcast(I32)[4 * q : 4 * q + 4, :], res_scales[:].bitcast(I32)[32 * q : 32 * q + 4, :]
            )
